import numpy as np
import ml_dtypes


def mxq(x, axis, fmt="e4m3"):
    dtype, down = {"e4m3": (ml_dtypes.float8_e4m3fn, 7), "e5m2": (ml_dtypes.float8_e5m2, 14)}[fmt]
    v = np.moveaxis(np.asarray(x, np.float32).astype(ml_dtypes.bfloat16).astype(np.float64), axis, -1)
    blocks = v.reshape(v.shape[:-1] + (-1, 32))
    amax = np.abs(blocks).max(-1, keepdims=True)
    byte = np.maximum(np.where(amax > 0, np.frexp(amax)[1] - 1 + 127, 0) - down, 1)
    scale = np.exp2(byte - 127.0)
    codes = (blocks / scale).astype(np.float32).astype(dtype).astype(np.float64)
    return np.moveaxis((codes * scale).reshape(v.shape), -1, axis)


WIDE = False


def mx_kscale(k):
    if not WIDE:
        return np.ones(k)
    levels = np.array([10, -10, 5, -5, 0])
    if k % 512:
        return np.exp2(np.random.permutation(np.resize(levels, k // 32))).repeat(32)
    a = np.empty((k // 512, 16))
    for p in range(k // 512):
        a[p, :8] = np.random.permutation(np.resize(levels, 8))
        for g in range(8):
            far = levels[np.abs(levels - a[p, g]) >= 10]
            a[p, g + 8] = far[np.random.randint(len(far))]
    return np.exp2(a.ravel()).repeat(32)


def f64(x):
    return np.asarray(x).astype(np.float64)


def striped(idx):
    return np.tile(np.asarray(idx).reshape(-1, 16).T, (8, 1)).astype(np.uint16)


def unstriped(offs):
    return offs[:16].T.reshape(-1).astype(np.int64)


def striped8(idx):
    return np.asarray(idx).reshape(8, -1, 16).transpose(0, 2, 1).reshape(128, -1).astype(np.uint16)


def unstriped8(offs):
    return offs.reshape(8, 16, -1).transpose(0, 2, 1).reshape(8, -1).astype(np.int64)


def pick8(x, idx, run):
    r = np.arange(len(x))
    return x[r[:, None], idx[r % (8 * run) // run]]


E2M1 = np.array([0.0, 0.5, 1.0, 1.5, 2.0, 3.0, 4.0, 6.0, -0.0, -0.5, -1.0, -1.5, -2.0, -3.0, -4.0, -6.0])


def pack_weight(w, fmt):
    k, n = w.shape
    w = f64(np.asarray(w, np.float32).astype(ml_dtypes.bfloat16)).reshape(k // 32, 32, n)
    amax = np.abs(w).max(1)
    if fmt == "e4m3":
        byte = np.frexp(amax)[1] - 1 + 127 - 7
    else:
        mant, ex = np.frexp(amax / 6.0)
        byte = np.where(mant > 0.5, ex, ex - 1) + 127
    byte = np.clip(np.where(amax > 0, byte, 1), 1, 254)
    scaled = (w * np.exp2(127.0 - byte)[:, None, :]).reshape(k, n).astype(np.float32)
    by_word = np.ascontiguousarray(scaled.reshape(k // 512, 128, 4, n).transpose(0, 1, 3, 2))
    if fmt == "e4m3":
        words = by_word.astype(ml_dtypes.float8_e4m3fn).view(np.uint8)
    else:
        c = by_word.astype(ml_dtypes.float4_e2m1fn).view(np.uint8) & 0xF
        words = (c[..., 0::2] | (c[..., 1::2] << 4)).reshape(k // 512, 128, 2 * n)
    return np.ascontiguousarray(words), np.ascontiguousarray(byte.astype(np.uint8).reshape(k // 512, 16, n))


def unpack_weight(words, scales, fmt):
    g, _, n = scales.shape
    words = np.ascontiguousarray(words).reshape(g, 128, n, -1)
    if fmt == "e4m3":
        vals = words.view(ml_dtypes.float8_e4m3fn).astype(np.float64)
    else:
        nib = np.empty((g, 128, n, 4), np.uint8)
        nib[..., 0::2] = words & 0xF
        nib[..., 1::2] = words >> 4
        vals = E2M1[nib]
    vals = vals * np.repeat(np.exp2(scales.astype(np.float64) - 127.0), 8, axis=1)[..., None]
    return vals.transpose(0, 1, 3, 2).reshape(g * 512, n)


def sigmoid(v):
    return 1.0 / (1.0 + np.exp(-v))


K, R, F, T, J, M, G = 512, 128, 512, 2048, 512, 256, 32


def setup_inputs():
    n = np.random.standard_normal
    idx = np.random.permutation(T)[:J]
    idx2 = np.stack([np.random.permutation(J)[:M] for _ in range(8)])
    fk = mx_kscale(K)
    dtabp = pack_weight(n((K, T)) / fk[:, None], "e4m3")
    tabp = pack_weight(n((K, T)) / fk[:, None], "e4m3")
    return {
        "dtab_words": dtabp[0],
        "dtab_scales": dtabp[1],
        "tab_words": tabp[0],
        "tab_scales": tabp[1],
        "w1": (n((K, R)) * 1 / np.sqrt(K) * fk[:, None]).astype(np.float32),
        "gain": (np.random.uniform(0.5, 1.5, (R, 1))).astype(np.float32),
        "pb": (np.random.uniform(-0.7, 0.7, (1, M))).astype(np.float32),
        "og": (np.random.uniform(0.5, 2.0, (R, 1))).astype(np.float32),
        "base": (0.3 * n((R, M))).astype(np.float32),
        "offs": striped(idx),
        "offs2": striped8(idx2),
    }


def reference(dtab_words, dtab_scales, tab_words, tab_scales, w1, gain, pb, og, base, offs, offs2):
    idx = unstriped(offs)
    idx2 = unstriped8(offs2)
    dtabu = unpack_weight(dtab_words, dtab_scales, "e4m3")
    tabu = unpack_weight(tab_words, tab_scales, "e4m3")
    w1q = mxq(f64(w1), 0, "e4m3")
    tabidxg = tabu[:, idx]
    a = w1q.T @ tabidxg
    dtabidxg = dtabu[:, idx]
    ta = w1q.T @ dtabidxg
    h1 = a * f64(gain)
    s = pick8(h1, idx2, 16) + f64(pb)
    q2 = np.sqrt(np.square(s).reshape(R, G, M // G).mean(axis=2) + 0.1)
    qr = np.repeat(q2, M // G, axis=1)
    xh1 = ta * f64(gain)
    xs = pick8(xh1, idx2, 16)
    xq2 = (xs * s * 2.0).reshape(R, G, M // G).mean(axis=2) * 0.5 / q2
    xqr = np.repeat(xq2, M // G, axis=1)
    xu1 = (xs - xqr * s / qr) / qr * sigmoid(s / qr) * (1.0 + s / qr * (1.0 - sigmoid(s / qr)))
    y = xu1 * f64(og) + f64(base)
    return y

@@ -1,0 +1,139 @@
+from contextlib import ExitStack
+
+import concourse.mybir as mybir
+
+F32 = mybir.dt.float32
+BF16 = mybir.dt.bfloat16
+I32 = mybir.dt.int32
+U32 = mybir.dt.uint32
+U16 = mybir.dt.uint16
+U8 = mybir.dt.uint8
+FP8X4 = mybir.dt.float8_e4m3fn_x4
+ALU = mybir.AluOpType
+ACT = mybir.ActivationFunctionType
+AX = mybir.AxisListType
+
+K, R, T, J, M, G = 512, 128, 2048, 512, 256, 32
+P = 128
+PACK = 4
+GROUP = M // G
+FLOPS = 2 * 2 * K * R * J
+
+
+def tile_attend_tcpickscaled_kernel(tc, dtab_words, dtab_scales, tab_words, tab_scales, w1, gain, pb, og, base, offs, offs2, out):
+    nc = tc.nc
+    with ExitStack() as ctx:
+        sb = ctx.enter_context(tc.tile_pool(name="sb", bufs=1))
+        ps = ctx.enter_context(tc.psum_pool(name="ps", bufs=1))
+
+        def grouped(t):
+            return t[:].rearrange("p (g i) -> p g i", i=GROUP)
+
+        def spread(t):
+            return t[:].unsqueeze(2).to_broadcast([P, G, GROUP])
+
+        def load_scales(tile, scales, first):
+            rows = scales[0].bitcast(I32)
+            for q in range(4):
+                nc.sync.dma_start(out=tile[32 * q + first : 32 * q + first + 4, :].bitcast(I32), in_=rows[4 * q : 4 * q + 4, :])
+
+        def load_words(tile, words):
+            nc.sync.dma_start(out=tile[:], in_=words[0].rearrange("p c t -> p (c t)").bitcast(I32))
+
+        slots = sb.tile([P, J // 16], U16, name="slots")
+        picks = sb.tile([P, M // 16], U16, name="picks")
+        tab_s = sb.tile([P, T], U8, name="tab_s", align_bytes=64)
+        dtab_s = sb.tile([P, T], U8, name="dtab_s", align_bytes=64)
+        tab_w = sb.tile([P, T], I32, name="tab_w", align_bytes=64)
+        dtab_w = sb.tile([P, T], I32, name="dtab_w", align_bytes=64)
+        w_raw = sb.tile([P, PACK, R], F32, name="w_raw")
+        gain_col = sb.tile([P, 1], F32, name="gain_col")
+        og_col = sb.tile([P, 1], F32, name="og_col")
+        pb_rows = sb.tile([P, M], F32, name="pb_rows")
+        base_sb = sb.tile([P, M], F32, name="base_sb")
+
+        nc.vector.memset(tab_s[:].bitcast(I32), 0)
+        nc.vector.memset(dtab_s[:].bitcast(I32), 0)
+
+        nc.sync.dma_start(slots[:], offs)
+        load_scales(tab_s, tab_scales, 0)
+        nc.sync.dma_start(out=w_raw[:], in_=w1.rearrange("(p t) r -> p t r", t=PACK))
+        load_words(tab_w, tab_words)
+        nc.sync.dma_start(picks[:], offs2)
+        load_scales(dtab_s, dtab_scales, 4)
+        load_words(dtab_w, dtab_words)
+        nc.gpsimd.dma_start(out=gain_col[:], in_=gain)
+        nc.sync.dma_start(out=pb_rows[:], in_=pb[0].partition_broadcast(P))
+        nc.gpsimd.dma_start(out=og_col[:], in_=og)
+        nc.sync.dma_start(out=base_sb[:], in_=base)
+
+        w_bf = sb.tile([P, R, PACK], BF16, name="w_bf", align_bytes=64)
+        nc.scalar.copy(out=w_bf[:], in_=w_raw[:].rearrange("p t r -> p r t"))
+        w_codes = sb.tile([P, R], U32, name="w_codes", align_bytes=64)
+        w_scales = sb.tile([P, R], U8, name="w_scales", align_bytes=64)
+
+        tab_sg = sb.tile([P, J], U8, name="tab_sg", align_bytes=64)
+        dtab_sg = sb.tile([P, J], U8, name="dtab_sg", align_bytes=64)
+        tab_wg = sb.tile([P, J], U32, name="tab_wg", align_bytes=64)
+        dtab_wg = sb.tile([P, J], U32, name="dtab_wg", align_bytes=64)
+
+        nc.vector.tensor_copy(tab_sg[:], tab_s[:].indirect(slots[:]))
+        nc.vector.quantize_mx(out=w_codes[:].bitcast(FP8X4), scales=w_scales[:], in_=w_bf[:].rearrange("p r t -> p (r t)"))
+        nc.vector.tensor_copy(tab_wg[:], tab_w[:].bitcast(U32).indirect(slots[:]))
+        a_ps = ps.tile([P, J], F32, name="a_ps")
+        nc.tensor.matmul_mx(out=a_ps[:], lhsT=w_codes[:].bitcast(FP8X4), lhsT_scale=w_scales[:],
+                            rhs=tab_wg[:].bitcast(FP8X4), rhs_scale=tab_sg[:], start=True, stop=True)
+        h1 = sb.tile([P, J], F32, name="h1")
+        nc.scalar.activation(out=h1[:], in_=a_ps[:], func=ACT.Copy, scale=gain_col[:])
+
+        nc.vector.tensor_copy(dtab_sg[:], dtab_s[:].indirect(slots[:]))
+        nc.vector.tensor_copy(dtab_wg[:], dtab_w[:].bitcast(U32).indirect(slots[:]))
+        ta_ps = ps.tile([P, J], F32, name="ta_ps")
+        nc.tensor.matmul_mx(out=ta_ps[:], lhsT=w_codes[:].bitcast(FP8X4), lhsT_scale=w_scales[:],
+                            rhs=dtab_wg[:].bitcast(FP8X4), rhs_scale=dtab_sg[4:P, :], start=True, stop=True)
+
+        s = sb.tile([P, M], F32, name="s")
+        nc.vector.tensor_tensor(s[:], h1[:].indirect(picks[:]), pb_rows[:], ALU.add)
+        sq = sb.tile([P, M], F32, name="sq")
+        nc.scalar.activation(out=sq[:], in_=s[:], func=ACT.Square)
+        xh1 = sb.tile([P, J], F32, name="xh1")
+        nc.scalar.activation(out=xh1[:], in_=ta_ps[:], func=ACT.Copy, scale=gain_col[:])
+        ssum = sb.tile([P, G], F32, name="ssum")
+        nc.vector.tensor_reduce(out=ssum[:], in_=grouped(sq), axis=AX.X, op=ALU.add)
+        q2 = sb.tile([P, G], F32, name="q2")
+        nc.scalar.activation(out=q2[:], in_=ssum[:], func=ACT.Sqrt, scale=1.0 / GROUP, bias=0.1)
+
+        xs = sb.tile([P, M], F32, name="xs")
+        nc.vector.tensor_copy(xs[:], xh1[:].indirect(picks[:]))
+        rq = sb.tile([P, G], F32, name="rq")
+        nc.vector.reciprocal(out=rq[:], in_=q2[:])
+        prod = sb.tile([P, M], F32, name="prod")
+        nc.vector.tensor_tensor(prod[:], xs[:], s[:], ALU.mult)
+        u = sb.tile([P, M], F32, name="u")
+        nc.vector.tensor_tensor(grouped(u), grouped(s), spread(rq), ALU.mult)
+        th = sb.tile([P, M], F32, name="th")
+        nc.scalar.activation(out=th[:], in_=u[:], func=ACT.Tanh, scale=0.5)
+        ns = sb.tile([P, M], F32, name="ns")
+        nc.scalar.activation(out=ns[:], in_=u[:], func=ACT.Silu, scale=-1.0)
+
+        csum = sb.tile([P, G], F32, name="csum")
+        nc.vector.tensor_reduce(out=csum[:], in_=grouped(prod), axis=AX.X, op=ALU.add)
+        r2 = sb.tile([P, G], F32, name="r2")
+        nc.vector.tensor_scalar(out=r2[:], in0=rq[:], scalar1=og_col[:], scalar2=-0.5, op0=ALU.mult, op1=ALU.mult)
+        rr = sb.tile([P, G], F32, name="rr")
+        nc.vector.scalar_tensor_tensor(out=rr[:], in0=rq[:], scalar=1.0 / GROUP, in1=r2[:], op0=ALU.mult, op1=ALU.mult)
+        xr = sb.tile([P, M], F32, name="xr")
+        nc.vector.tensor_tensor(grouped(xr), grouped(xs), spread(r2), ALU.mult)
+        kk = sb.tile([P, G], F32, name="kk")
+        nc.vector.tensor_tensor(kk[:], csum[:], rr[:], ALU.mult)
+        w = sb.tile([P, M], F32, name="w")
+        nc.vector.tensor_tensor(grouped(w), grouped(u), spread(kk), ALU.mult)
+        z = sb.tile([P, M], F32, name="z")
+        nc.vector.tensor_tensor(z[:], xr[:], w[:], ALU.subtract)
+        za = sb.tile([P, M], F32, name="za")
+        nc.vector.scalar_tensor_tensor(out=za[:], in0=th[:], scalar=1.0, in1=z[:], op0=ALU.add, op1=ALU.mult)
+        y = sb.tile([P, M], F32, name="y")
+        nc.vector.scalar_tensor_tensor(out=y[:], in0=ns[:], scalar=1.0, in1=za[:], op0=ALU.subtract, op1=ALU.mult)
+        res = sb.tile([P, M], F32, name="res")
+        nc.vector.tensor_tensor(res[:], y[:], base_sb[:], ALU.add)
+        nc.sync.dma_start(out=out, in_=res[:])

@@ -32,10 +32,10 @@ def tile_attend_tcpickscaled_kernel(tc, dtab_words, dtab_scales, tab_words, tab_
         def spread(t):
             return t[:].unsqueeze(2).to_broadcast([P, G, GROUP])
 
-        def load_scales(tile, scales, first):
+        def load_scales(tile, scales, first, queues):
             rows = scales[0].bitcast(I32)
-            for q in range(4):
-                nc.sync.dma_start(out=tile[32 * q + first : 32 * q + first + 4, :].bitcast(I32), in_=rows[4 * q : 4 * q + 4, :])
+            for q, queue in enumerate(queues):
+                queue.dma_start(out=tile[32 * q + first : 32 * q + first + 4, :].bitcast(I32), in_=rows[4 * q : 4 * q + 4, :])
 
         def load_words(tile, words):
             nc.sync.dma_start(out=tile[:], in_=words[0].rearrange("p c t -> p (c t)").bitcast(I32))
@@ -43,97 +43,116 @@ def tile_attend_tcpickscaled_kernel(tc, dtab_words, dtab_scales, tab_words, tab_
         slots = sb.tile([P, J // 16], U16, name="slots")
         picks = sb.tile([P, M // 16], U16, name="picks")
         tab_s = sb.tile([P, T], U8, name="tab_s", align_bytes=64)
-        dtab_s = sb.tile([P, T], U8, name="dtab_s", align_bytes=64)
-        tab_w = sb.tile([P, T], I32, name="tab_w", align_bytes=64)
-        dtab_w = sb.tile([P, T], I32, name="dtab_w", align_bytes=64)
-        w_raw = sb.tile([P, PACK, R], F32, name="w_raw")
+        dtab_s = sb.tile([P, T], U8, name="dtab_s", tag="late_bytes", align_bytes=64)
+        one = sb.tile([P, 1], F32, name="one", tag="first_words", align_bytes=64)
+        eps = sb.tile([P, 1], F32, name="eps")
+        w_raw = sb.tile([P, PACK, R], F32, name="w_raw", tag="late_words", align_bytes=64)
         gain_col = sb.tile([P, 1], F32, name="gain_col")
         og_col = sb.tile([P, 1], F32, name="og_col")
-        pb_rows = sb.tile([P, M], F32, name="pb_rows")
+        pb_rows = sb.tile([P, M], F32, name="pb_rows", tag="bias_rows", align_bytes=64)
         base_sb = sb.tile([P, M], F32, name="base_sb")
 
+        nc.vector.memset(one[:], 1.0)
         nc.vector.memset(tab_s[:].bitcast(I32), 0)
+        nc.vector.tensor_scalar(out=eps[:], in0=one[:], scalar1=0.1, scalar2=None, op0=ALU.mult)
         nc.vector.memset(dtab_s[:].bitcast(I32), 0)
 
         nc.sync.dma_start(slots[:], offs)
-        load_scales(tab_s, tab_scales, 0)
-        nc.sync.dma_start(out=w_raw[:], in_=w1.rearrange("(p t) r -> p t r", t=PACK))
-        load_words(tab_w, tab_words)
         nc.sync.dma_start(picks[:], offs2)
-        load_scales(dtab_s, dtab_scales, 4)
-        load_words(dtab_w, dtab_words)
+        nc.sync.dma_start(out=w_raw[:], in_=w1.rearrange("(p t) r -> p t r", t=PACK))
+        load_scales(tab_s, tab_scales, 0, [nc.sync] * 4)
+        tab_w = sb.tile([P, T], I32, name="tab_w", tag="first_words", align_bytes=64)
+        load_words(tab_w, tab_words)
+        warm_out = sb.tile([P, 1], F32, name="warm_out")
+        nc.scalar.activation(out=warm_out[:], in_=eps[:], func=ACT.Abs_reciprocal_sqrt)
+        load_scales(dtab_s, dtab_scales, 4, [nc.sync] * 4)
         nc.gpsimd.dma_start(out=gain_col[:], in_=gain)
-        nc.sync.dma_start(out=pb_rows[:], in_=pb[0].partition_broadcast(P))
+        nc.gpsimd.dma_start(out=pb_rows[:], in_=pb[0].partition_broadcast(P))
         nc.gpsimd.dma_start(out=og_col[:], in_=og)
-        nc.sync.dma_start(out=base_sb[:], in_=base)
+        nc.gpsimd.dma_start(out=base_sb[:], in_=base)
 
         w_bf = sb.tile([P, R, PACK], BF16, name="w_bf", align_bytes=64)
-        nc.scalar.copy(out=w_bf[:], in_=w_raw[:].rearrange("p t r -> p r t"))
+        nc.vector.tensor_copy(out=w_bf[:], in_=w_raw[:].rearrange("p t r -> p r t"))
+        dtab_w = sb.tile([P, T], I32, name="dtab_w", tag="late_words", align_bytes=64)
+        load_words(dtab_w, dtab_words)
         w_codes = sb.tile([P, R], U32, name="w_codes", align_bytes=64)
         w_scales = sb.tile([P, R], U8, name="w_scales", align_bytes=64)
 
         tab_sg = sb.tile([P, J], U8, name="tab_sg", align_bytes=64)
         dtab_sg = sb.tile([P, J], U8, name="dtab_sg", align_bytes=64)
         tab_wg = sb.tile([P, J], U32, name="tab_wg", align_bytes=64)
-        dtab_wg = sb.tile([P, J], U32, name="dtab_wg", align_bytes=64)
+
 
         nc.vector.tensor_copy(tab_sg[:], tab_s[:].indirect(slots[:]))
         nc.vector.quantize_mx(out=w_codes[:].bitcast(FP8X4), scales=w_scales[:], in_=w_bf[:].rearrange("p r t -> p (r t)"))
-        nc.vector.tensor_copy(tab_wg[:], tab_w[:].bitcast(U32).indirect(slots[:]))
-        a_ps = ps.tile([P, J], F32, name="a_ps")
-        nc.tensor.matmul_mx(out=a_ps[:], lhsT=w_codes[:].bitcast(FP8X4), lhsT_scale=w_scales[:],
-                            rhs=tab_wg[:].bitcast(FP8X4), rhs_scale=tab_sg[:], start=True, stop=True)
         h1 = sb.tile([P, J], F32, name="h1")
-        nc.scalar.activation(out=h1[:], in_=a_ps[:], func=ACT.Copy, scale=gain_col[:])
+        xh1 = sb.tile([P, J], F32, name="xh1")
+
+        def gather_half(dst, table, h):
+            cols = slice(h * J // 2, (h + 1) * J // 2)
+            nc.vector.tensor_copy(dst[:, cols], table[:].bitcast(U32).indirect(slots[:, h * J // 32 : (h + 1) * J // 32]))
+
+        def product_half(dst, words, scales, h, name):
+            cols = slice(h * J // 2, (h + 1) * J // 2)
+            acc = ps.tile([P, J // 2], F32, name=name)
+            nc.tensor.matmul_mx(out=acc[:], lhsT=w_codes[:].bitcast(FP8X4), lhsT_scale=w_scales[:],
+                                rhs=words[:, cols].bitcast(FP8X4), rhs_scale=scales[:, cols], start=True, stop=True)
+            nc.scalar.activation(out=dst[:, cols], in_=acc[:], func=ACT.Copy, scale=gain_col[:])
+
+        for h in range(2):
+            gather_half(tab_wg, tab_w, h)
+            product_half(h1, tab_wg, tab_sg[:], h, f"a_ps{h}")
 
         nc.vector.tensor_copy(dtab_sg[:], dtab_s[:].indirect(slots[:]))
-        nc.vector.tensor_copy(dtab_wg[:], dtab_w[:].bitcast(U32).indirect(slots[:]))
-        ta_ps = ps.tile([P, J], F32, name="ta_ps")
-        nc.tensor.matmul_mx(out=ta_ps[:], lhsT=w_codes[:].bitcast(FP8X4), lhsT_scale=w_scales[:],
-                            rhs=dtab_wg[:].bitcast(FP8X4), rhs_scale=dtab_sg[4:P, :], start=True, stop=True)
-
-        s = sb.tile([P, M], F32, name="s")
+        s = sb.tile([P, M], F32, name="s", tag="late_bytes", align_bytes=64)
         nc.vector.tensor_tensor(s[:], h1[:].indirect(picks[:]), pb_rows[:], ALU.add)
         sq = sb.tile([P, M], F32, name="sq")
         nc.scalar.activation(out=sq[:], in_=s[:], func=ACT.Square)
-        xh1 = sb.tile([P, J], F32, name="xh1")
-        nc.scalar.activation(out=xh1[:], in_=ta_ps[:], func=ACT.Copy, scale=gain_col[:])
-        ssum = sb.tile([P, G], F32, name="ssum")
+        dtab_wg = sb.tile([P, J], U32, name="dtab_wg", tag="bias_rows", align_bytes=64)
+        gather_half(dtab_wg, dtab_w, 0)
+        gather_half(dtab_wg, dtab_w, 1)
+        product_half(xh1, dtab_wg, dtab_sg[4:P, :], 0, "ta_ps0")
+        ssum = sb.tile([P, G], F32, name="ssum", tag="late_words", align_bytes=64)
         nc.vector.tensor_reduce(out=ssum[:], in_=grouped(sq), axis=AX.X, op=ALU.add)
-        q2 = sb.tile([P, G], F32, name="q2")
-        nc.scalar.activation(out=q2[:], in_=ssum[:], func=ACT.Sqrt, scale=1.0 / GROUP, bias=0.1)
-
-        xs = sb.tile([P, M], F32, name="xs")
-        nc.vector.tensor_copy(xs[:], xh1[:].indirect(picks[:]))
         rq = sb.tile([P, G], F32, name="rq")
-        nc.vector.reciprocal(out=rq[:], in_=q2[:])
-        prod = sb.tile([P, M], F32, name="prod")
-        nc.vector.tensor_tensor(prod[:], xs[:], s[:], ALU.mult)
+        nc.scalar.activation(out=rq[:], in_=ssum[:], func=ACT.Abs_reciprocal_sqrt, scale=1.0 / GROUP, bias=eps[:])
+        product_half(xh1, dtab_wg, dtab_sg[4:P, :], 1, "ta_ps1")
         u = sb.tile([P, M], F32, name="u")
         nc.vector.tensor_tensor(grouped(u), grouped(s), spread(rq), ALU.mult)
-        th = sb.tile([P, M], F32, name="th")
-        nc.scalar.activation(out=th[:], in_=u[:], func=ACT.Tanh, scale=0.5)
+        rwide = sb.tile([P, M], F32, name="rwide")
+        nc.vector.tensor_scalar(out=grouped(rwide), in0=spread(rq), scalar1=og_col[:], scalar2=None, op0=ALU.mult)
         ns = sb.tile([P, M], F32, name="ns")
         nc.scalar.activation(out=ns[:], in_=u[:], func=ACT.Silu, scale=-1.0)
+        th = sb.tile([P, M], F32, name="th")
+        nc.scalar.activation(out=th[:], in_=u[:], func=ACT.Tanh, scale=0.5)
 
-        csum = sb.tile([P, G], F32, name="csum")
-        nc.vector.tensor_reduce(out=csum[:], in_=grouped(prod), axis=AX.X, op=ALU.add)
-        r2 = sb.tile([P, G], F32, name="r2")
-        nc.vector.tensor_scalar(out=r2[:], in0=rq[:], scalar1=og_col[:], scalar2=-0.5, op0=ALU.mult, op1=ALU.mult)
-        rr = sb.tile([P, G], F32, name="rr")
-        nc.vector.scalar_tensor_tensor(out=rr[:], in0=rq[:], scalar=1.0 / GROUP, in1=r2[:], op0=ALU.mult, op1=ALU.mult)
         xr = sb.tile([P, M], F32, name="xr")
-        nc.vector.tensor_tensor(grouped(xr), grouped(xs), spread(r2), ALU.mult)
-        kk = sb.tile([P, G], F32, name="kk")
-        nc.vector.tensor_tensor(kk[:], csum[:], rr[:], ALU.mult)
+        prod = sb.tile([P, M], F32, name="prod")
+        csum = sb.tile([P, G], F32, name="csum")
+        for h in range(2):
+            c = slice(h * M // 2, (h + 1) * M // 2)
+            nc.vector.tensor_tensor(xr[:, c], xh1[:].indirect(picks[:, h * M // 32 : (h + 1) * M // 32]), rwide[:, c], ALU.mult)
+        for h in range(2):
+            c = slice(h * M // 2, (h + 1) * M // 2)
+            nc.vector.tensor_tensor(prod[:, c], xr[:, c], u[:, c], ALU.mult)
+        for h in range(2):
+            gs = slice(h * G // 2, (h + 1) * G // 2)
+            nc.vector.tensor_reduce(out=csum[:, gs], in_=grouped(prod)[:, gs, :], axis=AX.X, op=ALU.add)
+        halves = [slice(0, M // 2), slice(M // 2, M)]
         w = sb.tile([P, M], F32, name="w")
-        nc.vector.tensor_tensor(grouped(w), grouped(u), spread(kk), ALU.mult)
         z = sb.tile([P, M], F32, name="z")
-        nc.vector.tensor_tensor(z[:], xr[:], w[:], ALU.subtract)
         za = sb.tile([P, M], F32, name="za")
-        nc.vector.scalar_tensor_tensor(out=za[:], in0=th[:], scalar=1.0, in1=z[:], op0=ALU.add, op1=ALU.mult)
         y = sb.tile([P, M], F32, name="y")
-        nc.vector.scalar_tensor_tensor(out=y[:], in0=ns[:], scalar=1.0, in1=za[:], op0=ALU.subtract, op1=ALU.mult)
         res = sb.tile([P, M], F32, name="res")
-        nc.vector.tensor_tensor(res[:], y[:], base_sb[:], ALU.add)
-        nc.sync.dma_start(out=out, in_=res[:])
+        for h in range(2):
+            gs = slice(h * G // 2, (h + 1) * G // 2)
+            nc.vector.scalar_tensor_tensor(out=grouped(w)[:, gs, :], in0=grouped(u)[:, gs, :], scalar=1.0 / GROUP, in1=spread(csum)[:, gs, :], op0=ALU.mult, op1=ALU.mult)
+        for c in halves:
+            nc.vector.tensor_tensor(z[:, c], xr[:, c], w[:, c], ALU.subtract)
+        for c in halves:
+            nc.vector.scalar_tensor_tensor(out=za[:, c], in0=ns[:, c], scalar=1.0, in1=z[:, c], op0=ALU.subtract, op1=ALU.mult)
+        for c in halves:
+            nc.vector.scalar_tensor_tensor(out=y[:, c], in0=th[:, c], scalar=1.0, in1=za[:, c], op0=ALU.add, op1=ALU.mult)
+        for c, queue in zip(halves, (nc.sync, nc.scalar)):
+            nc.vector.scalar_tensor_tensor(out=res[:, c], in0=y[:, c], scalar=-0.5, in1=base_sb[:, c], op0=ALU.mult, op1=ALU.add)
+            queue.dma_start(out=out[:, c], in_=res[:, c])

@@ -17,14 +17,23 @@ K, R, T, J, M, G = 512, 128, 2048, 512, 256, 32
 P = 128
 PACK = 4
 GROUP = M // G
+LIST_ROWS = 16
+QUADRANT = 32
+DTAB_FIRST = 4
+EPS = 0.1
 FLOPS = 2 * 2 * K * R * J
 
 
-def tile_attend_tcpickscaled_kernel(tc, dtab_words, dtab_scales, tab_words, tab_scales, w1, gain, pb, og, base, offs, offs2, out):
+def tile_attend_tcpickscaled_kernel(
+    tc, dtab_words, dtab_scales, tab_words, tab_scales, w1, gain, pb, og, base, offs, offs2, out
+):
     nc = tc.nc
     with ExitStack() as ctx:
         sb = ctx.enter_context(tc.tile_pool(name="sb", bufs=1))
         ps = ctx.enter_context(tc.psum_pool(name="ps", bufs=1))
+
+        def half(h, width):
+            return slice(h * width // 2, (h + 1) * width // 2)
 
         def grouped(t):
             return t[:].rearrange("p (g i) -> p g i", i=GROUP)
@@ -32,44 +41,51 @@ def tile_attend_tcpickscaled_kernel(tc, dtab_words, dtab_scales, tab_words, tab_
         def spread(t):
             return t[:].unsqueeze(2).to_broadcast([P, G, GROUP])
 
-        def load_scales(tile, scales, first, queues):
+        def load_scales(tile, scales, first):
             rows = scales[0].bitcast(I32)
-            for q, queue in enumerate(queues):
-                queue.dma_start(out=tile[32 * q + first : 32 * q + first + 4, :].bitcast(I32), in_=rows[4 * q : 4 * q + 4, :])
+            for q in range(P // QUADRANT):
+                start = QUADRANT * q + first
+                nc.sync.dma_start(out=tile[start : start + 4, :].bitcast(I32), in_=rows[4 * q : 4 * q + 4, :])
 
         def load_words(tile, words):
             nc.sync.dma_start(out=tile[:], in_=words[0].rearrange("p c t -> p (c t)").bitcast(I32))
 
-        slots = sb.tile([P, J // 16], U16, name="slots")
-        picks = sb.tile([P, M // 16], U16, name="picks")
+        slots = sb.tile([P, J // LIST_ROWS], U16, name="slots")
+        picks = sb.tile([P, M // LIST_ROWS], U16, name="picks")
         tab_s = sb.tile([P, T], U8, name="tab_s", align_bytes=64)
         dtab_s = sb.tile([P, T], U8, name="dtab_s", tag="late_bytes", align_bytes=64)
         one = sb.tile([P, 1], F32, name="one", tag="first_words", align_bytes=64)
         eps = sb.tile([P, 1], F32, name="eps")
         w_raw = sb.tile([P, PACK, R], F32, name="w_raw", tag="late_words", align_bytes=64)
-        gain_col = sb.tile([P, 1], F32, name="gain_col")
-        og_col = sb.tile([P, 1], F32, name="og_col")
         pb_rows = sb.tile([P, M], F32, name="pb_rows", tag="bias_rows", align_bytes=64)
-        base_sb = sb.tile([P, M], F32, name="base_sb")
 
         nc.vector.memset(one[:], 1.0)
         nc.vector.memset(tab_s[:].bitcast(I32), 0)
-        nc.vector.tensor_scalar(out=eps[:], in0=one[:], scalar1=0.1, scalar2=None, op0=ALU.mult)
+        nc.vector.tensor_scalar(out=eps[:], in0=one[:], scalar1=4 * EPS, scalar2=None, op0=ALU.mult)
         nc.vector.memset(dtab_s[:].bitcast(I32), 0)
 
         nc.sync.dma_start(slots[:], offs)
         nc.sync.dma_start(picks[:], offs2)
         nc.sync.dma_start(out=w_raw[:], in_=w1.rearrange("(p t) r -> p t r", t=PACK))
-        load_scales(tab_s, tab_scales, 0, [nc.sync] * 4)
+        load_scales(tab_s, tab_scales, 0)
         tab_w = sb.tile([P, T], I32, name="tab_w", tag="first_words", align_bytes=64)
         load_words(tab_w, tab_words)
+
+        ident = sb.tile([P, P], F32, name="ident")
+        zeros = sb.tile([P, P], F32, name="zeros", tag="columns")
+        nc.gpsimd.memset(zeros[:], 0.0)
+        nc.gpsimd.affine_select(
+            out=ident[:], in_=zeros[:], compare_op=ALU.not_equal, fill=1.0, base=0, pattern=[[-1, P]], channel_multiplier=1
+        )
+
         warm_out = sb.tile([P, 1], F32, name="warm_out")
         nc.scalar.activation(out=warm_out[:], in_=eps[:], func=ACT.Abs_reciprocal_sqrt)
-        load_scales(dtab_s, dtab_scales, 4, [nc.sync] * 4)
-        nc.gpsimd.dma_start(out=gain_col[:], in_=gain)
-        nc.gpsimd.dma_start(out=pb_rows[:], in_=pb[0].partition_broadcast(P))
-        nc.gpsimd.dma_start(out=og_col[:], in_=og)
-        nc.gpsimd.dma_start(out=base_sb[:], in_=base)
+
+        columns = sb.tile([P, 2, 8], F32, name="columns", tag="columns")
+        gain_col, pb_pairs = columns[:, 0, 0:1], columns[:, 1, 0:2]
+        load_scales(dtab_s, dtab_scales, DTAB_FIRST)
+        nc.sync.dma_start(out=gain_col, in_=gain)
+        nc.sync.dma_start(out=pb_pairs, in_=pb[0].rearrange("(p c) -> p c", c=2))
 
         w_bf = sb.tile([P, R, PACK], BF16, name="w_bf", align_bytes=64)
         nc.vector.tensor_copy(out=w_bf[:], in_=w_raw[:].rearrange("p t r -> p r t"))
@@ -80,28 +96,46 @@ def tile_attend_tcpickscaled_kernel(tc, dtab_words, dtab_scales, tab_words, tab_
 
         tab_sg = sb.tile([P, J], U8, name="tab_sg", align_bytes=64)
         dtab_sg = sb.tile([P, J], U8, name="dtab_sg", align_bytes=64)
-        tab_wg = sb.tile([P, J], U32, name="tab_wg", align_bytes=64)
-
+        tab_wg = sb.tile([P, J], U32, name="tab_wg", tag="first_picked", align_bytes=64)
 
         nc.vector.tensor_copy(tab_sg[:], tab_s[:].indirect(slots[:]))
-        nc.vector.quantize_mx(out=w_codes[:].bitcast(FP8X4), scales=w_scales[:], in_=w_bf[:].rearrange("p r t -> p (r t)"))
+        nc.vector.quantize_mx(
+            out=w_codes[:].bitcast(FP8X4), scales=w_scales[:], in_=w_bf[:].rearrange("p r t -> p (r t)")
+        )
+
+        pb_ps = ps.tile([P, 2, P], F32, name="pb_ps")
+        for c in range(2):
+            nc.tensor.transpose(pb_ps[:, c, :], pb_pairs[:, c : c + 1].to_broadcast([P, P]), ident[:])
+        nc.scalar.copy(out=pb_rows[:].rearrange("p (j c) -> p j c", c=2), in_=pb_ps[:].rearrange("p c j -> p j c"))
+
         h1 = sb.tile([P, J], F32, name="h1")
         xh1 = sb.tile([P, J], F32, name="xh1")
 
-        def gather_half(dst, table, h):
-            cols = slice(h * J // 2, (h + 1) * J // 2)
-            nc.vector.tensor_copy(dst[:, cols], table[:].bitcast(U32).indirect(slots[:, h * J // 32 : (h + 1) * J // 32]))
+        def gather_words(dst, table, h):
+            nc.vector.tensor_copy(dst[:, half(h, J)], table[:].bitcast(U32).indirect(slots[:, half(h, J // LIST_ROWS)]))
 
-        def product_half(dst, words, scales, h, name):
-            cols = slice(h * J // 2, (h + 1) * J // 2)
+        def product(words, scales, h, name):
             acc = ps.tile([P, J // 2], F32, name=name)
-            nc.tensor.matmul_mx(out=acc[:], lhsT=w_codes[:].bitcast(FP8X4), lhsT_scale=w_scales[:],
-                                rhs=words[:, cols].bitcast(FP8X4), rhs_scale=scales[:, cols], start=True, stop=True)
-            nc.scalar.activation(out=dst[:, cols], in_=acc[:], func=ACT.Copy, scale=gain_col[:])
+            nc.tensor.matmul_mx(
+                out=acc[:],
+                lhsT=w_codes[:].bitcast(FP8X4),
+                lhsT_scale=w_scales[:],
+                rhs=words[:, half(h, J)].bitcast(FP8X4),
+                rhs_scale=scales[:, half(h, J)],
+                start=True,
+                stop=True,
+            )
+            return acc
 
         for h in range(2):
-            gather_half(tab_wg, tab_w, h)
-            product_half(h1, tab_wg, tab_sg[:], h, f"a_ps{h}")
+            gather_words(tab_wg, tab_w, h)
+            a_half = product(tab_wg, tab_sg[:], h, f"a_ps{h}")
+            nc.scalar.activation(out=h1[:, half(h, J)], in_=a_half[:], func=ACT.Copy, scale=gain_col)
+
+        og_col = sb.tile([P, 1], F32, name="og_col", tag="first_words", align_bytes=64)
+        nc.sync.dma_start(out=og_col[:], in_=og)
+        base_sb = sb.tile([P, M], F32, name="base_sb", tag="first_picked", align_bytes=64)
+        nc.sync.dma_start(out=base_sb[:], in_=base)
 
         nc.vector.tensor_copy(dtab_sg[:], dtab_s[:].indirect(slots[:]))
         s = sb.tile([P, M], F32, name="s", tag="late_bytes", align_bytes=64)
@@ -109,50 +143,63 @@ def tile_attend_tcpickscaled_kernel(tc, dtab_words, dtab_scales, tab_words, tab_
         sq = sb.tile([P, M], F32, name="sq")
         nc.scalar.activation(out=sq[:], in_=s[:], func=ACT.Square)
         dtab_wg = sb.tile([P, J], U32, name="dtab_wg", tag="bias_rows", align_bytes=64)
-        gather_half(dtab_wg, dtab_w, 0)
-        gather_half(dtab_wg, dtab_w, 1)
-        product_half(xh1, dtab_wg, dtab_sg[4:P, :], 0, "ta_ps0")
-        ssum = sb.tile([P, G], F32, name="ssum", tag="late_words", align_bytes=64)
-        nc.vector.tensor_reduce(out=ssum[:], in_=grouped(sq), axis=AX.X, op=ALU.add)
-        rq = sb.tile([P, G], F32, name="rq")
-        nc.scalar.activation(out=rq[:], in_=ssum[:], func=ACT.Abs_reciprocal_sqrt, scale=1.0 / GROUP, bias=eps[:])
-        product_half(xh1, dtab_wg, dtab_sg[4:P, :], 1, "ta_ps1")
+        gather_words(dtab_wg, dtab_w, 0)
+        gather_words(dtab_wg, dtab_w, 1)
+        ta_first = product(dtab_wg, dtab_sg[DTAB_FIRST:P, :], 0, "ta_ps0")
+        nc.scalar.activation(out=xh1[:, half(0, J)], in_=ta_first[:], func=ACT.Copy, scale=gain_col)
+        sq_sum = sb.tile([P, G], F32, name="sq_sum", tag="late_words", align_bytes=64)
+        nc.vector.tensor_reduce(out=sq_sum[:], in_=grouped(sq), axis=AX.X, op=ALU.add)
+        half_inv_q = sb.tile([P, M], F32, name="half_inv_q")
+        nc.scalar.activation(
+            out=grouped(half_inv_q), in_=spread(sq_sum), func=ACT.Abs_reciprocal_sqrt, scale=4.0 / GROUP, bias=eps[:]
+        )
+        ta_second = product(dtab_wg, dtab_sg[DTAB_FIRST:P, :], 1, "ta_ps1")
+        nc.vector.tensor_scalar(out=xh1[:, half(1, J)], in0=ta_second[:], scalar1=gain_col, scalar2=None, op0=ALU.mult)
+
         u = sb.tile([P, M], F32, name="u")
-        nc.vector.tensor_tensor(grouped(u), grouped(s), spread(rq), ALU.mult)
-        rwide = sb.tile([P, M], F32, name="rwide")
-        nc.vector.tensor_scalar(out=grouped(rwide), in0=spread(rq), scalar1=og_col[:], scalar2=None, op0=ALU.mult)
-        ns = sb.tile([P, M], F32, name="ns")
-        nc.scalar.activation(out=ns[:], in_=u[:], func=ACT.Silu, scale=-1.0)
-        th = sb.tile([P, M], F32, name="th")
-        nc.scalar.activation(out=th[:], in_=u[:], func=ACT.Tanh, scale=0.5)
+        nc.vector.scalar_tensor_tensor(out=u[:], in0=s[:], scalar=2.0, in1=half_inv_q[:], op0=ALU.mult, op1=ALU.mult)
+        silu_neg = sb.tile([P, M], F32, name="silu_neg")
+        nc.scalar.activation(out=silu_neg[:], in_=u[:], func=ACT.Silu, scale=-1.0)
+        tanh_half = sb.tile([P, M], F32, name="tanh_half")
+        nc.scalar.activation(out=tanh_half[:], in_=u[:], func=ACT.Tanh, scale=0.5)
 
         xr = sb.tile([P, M], F32, name="xr")
-        prod = sb.tile([P, M], F32, name="prod")
-        csum = sb.tile([P, G], F32, name="csum")
+        xr_u = sb.tile([P, M], F32, name="xr_u")
+        xr_u_sum = sb.tile([P, G], F32, name="xr_u_sum")
         for h in range(2):
-            c = slice(h * M // 2, (h + 1) * M // 2)
-            nc.vector.tensor_tensor(xr[:, c], xh1[:].indirect(picks[:, h * M // 32 : (h + 1) * M // 32]), rwide[:, c], ALU.mult)
+            nc.vector.tensor_tensor(
+                xr[:, half(h, M)], xh1[:].indirect(picks[:, half(h, M // LIST_ROWS)]), half_inv_q[:, half(h, M)], ALU.mult
+            )
         for h in range(2):
-            c = slice(h * M // 2, (h + 1) * M // 2)
-            nc.vector.tensor_tensor(prod[:, c], xr[:, c], u[:, c], ALU.mult)
+            nc.vector.tensor_tensor(xr_u[:, half(h, M)], xr[:, half(h, M)], u[:, half(h, M)], ALU.mult)
         for h in range(2):
-            gs = slice(h * G // 2, (h + 1) * G // 2)
-            nc.vector.tensor_reduce(out=csum[:, gs], in_=grouped(prod)[:, gs, :], axis=AX.X, op=ALU.add)
-        halves = [slice(0, M // 2), slice(M // 2, M)]
-        w = sb.tile([P, M], F32, name="w")
-        z = sb.tile([P, M], F32, name="z")
-        za = sb.tile([P, M], F32, name="za")
-        y = sb.tile([P, M], F32, name="y")
+            nc.vector.tensor_reduce(out=xr_u_sum[:, half(h, G)], in_=grouped(xr_u)[:, half(h, G), :], axis=AX.X, op=ALU.add)
+        along_u = sb.tile([P, M], F32, name="along_u")
+        neg_xu = sb.tile([P, M], F32, name="neg_xu")
+        neg_slope = sb.tile([P, M], F32, name="neg_slope")
+        xu1 = sb.tile([P, M], F32, name="xu1")
         res = sb.tile([P, M], F32, name="res")
         for h in range(2):
-            gs = slice(h * G // 2, (h + 1) * G // 2)
-            nc.vector.scalar_tensor_tensor(out=grouped(w)[:, gs, :], in0=grouped(u)[:, gs, :], scalar=1.0 / GROUP, in1=spread(csum)[:, gs, :], op0=ALU.mult, op1=ALU.mult)
-        for c in halves:
-            nc.vector.tensor_tensor(z[:, c], xr[:, c], w[:, c], ALU.subtract)
-        for c in halves:
-            nc.vector.scalar_tensor_tensor(out=za[:, c], in0=ns[:, c], scalar=1.0, in1=z[:, c], op0=ALU.subtract, op1=ALU.mult)
-        for c in halves:
-            nc.vector.scalar_tensor_tensor(out=y[:, c], in0=th[:, c], scalar=1.0, in1=za[:, c], op0=ALU.add, op1=ALU.mult)
-        for c, queue in zip(halves, (nc.sync, nc.scalar)):
-            nc.vector.scalar_tensor_tensor(out=res[:, c], in0=y[:, c], scalar=-0.5, in1=base_sb[:, c], op0=ALU.mult, op1=ALU.add)
-            queue.dma_start(out=out[:, c], in_=res[:, c])
+            nc.vector.scalar_tensor_tensor(
+                out=grouped(along_u)[:, half(h, G), :],
+                in0=grouped(u)[:, half(h, G), :],
+                scalar=1.0 / GROUP,
+                in1=spread(xr_u_sum)[:, half(h, G), :],
+                op0=ALU.mult,
+                op1=ALU.mult,
+            )
+        for h in range(2):
+            nc.vector.tensor_tensor(neg_xu[:, half(h, M)], along_u[:, half(h, M)], xr[:, half(h, M)], ALU.subtract)
+        tanh_plus_one = sb.tile([P, M], F32, name="tanh_plus_one")
+        nc.scalar.activation(out=tanh_plus_one[:], in_=tanh_half[:], func=ACT.Identity, bias=1.0)
+        nc.vector.scalar_tensor_tensor(
+            out=neg_slope[:], in0=silu_neg[:], scalar=1.0, in1=tanh_plus_one[:], op0=ALU.subtract, op1=ALU.mult
+        )
+        for h in range(2):
+            nc.vector.tensor_tensor(xu1[:, half(h, M)], neg_xu[:, half(h, M)], neg_slope[:, half(h, M)], ALU.mult)
+        for h, queue in enumerate((nc.sync, nc.scalar)):
+            cols = half(h, M)
+            nc.vector.scalar_tensor_tensor(
+                out=res[:, cols], in0=xu1[:, cols], scalar=og_col[:], in1=base_sb[:, cols], op0=ALU.mult, op1=ALU.add
+            )
+            queue.dma_start(out=out[:, cols], in_=res[:, cols])

from contextlib import ExitStack

import concourse.mybir as mybir

F32 = mybir.dt.float32
BF16 = mybir.dt.bfloat16
I32 = mybir.dt.int32
U32 = mybir.dt.uint32
U16 = mybir.dt.uint16
U8 = mybir.dt.uint8
FP8X4 = mybir.dt.float8_e4m3fn_x4
ALU = mybir.AluOpType
ACT = mybir.ActivationFunctionType
AX = mybir.AxisListType

K, R, T, J, M, G = 512, 128, 2048, 512, 256, 32
P = 128
PACK = 4
GROUP = M // G
LIST_ROWS = 16
QUADRANT = 32
DTAB_FIRST = 4
EPS = 0.1
FLOPS = 2 * 2 * K * R * J


def tile_attend_tcpickscaled_kernel(
    tc, dtab_words, dtab_scales, tab_words, tab_scales, w1, gain, pb, og, base, offs, offs2, out
):
    nc = tc.nc
    with ExitStack() as ctx:
        sb = ctx.enter_context(tc.tile_pool(name="sb", bufs=1))
        ps = ctx.enter_context(tc.psum_pool(name="ps", bufs=1))

        def half(h, width):
            return slice(h * width // 2, (h + 1) * width // 2)

        def grouped(t):
            return t[:].rearrange("p (g i) -> p g i", i=GROUP)

        def spread(t):
            return t[:].unsqueeze(2).to_broadcast([P, G, GROUP])

        def load_scales(tile, scales, first):
            rows = scales[0].bitcast(I32)
            for q in range(P // QUADRANT):
                start = QUADRANT * q + first
                nc.sync.dma_start(out=tile[start : start + 4, :].bitcast(I32), in_=rows[4 * q : 4 * q + 4, :])

        def load_words(tile, words):
            nc.sync.dma_start(out=tile[:], in_=words[0].rearrange("p c t -> p (c t)").bitcast(I32))

        slots = sb.tile([P, J // LIST_ROWS], U16, name="slots")
        picks = sb.tile([P, M // LIST_ROWS], U16, name="picks")
        tab_s = sb.tile([P, T], U8, name="tab_s", align_bytes=64)
        dtab_s = sb.tile([P, T], U8, name="dtab_s", tag="late_bytes", align_bytes=64)
        one = sb.tile([P, 1], F32, name="one", tag="first_words", align_bytes=64)
        eps = sb.tile([P, 1], F32, name="eps")
        w_raw = sb.tile([P, PACK, R], F32, name="w_raw", tag="late_words", align_bytes=64)
        pb_rows = sb.tile([P, M], F32, name="pb_rows", tag="bias_rows", align_bytes=64)

        nc.vector.memset(one[:], 1.0)
        nc.vector.memset(tab_s[:].bitcast(I32), 0)
        nc.vector.tensor_scalar(out=eps[:], in0=one[:], scalar1=4 * EPS, scalar2=None, op0=ALU.mult)
        nc.vector.memset(dtab_s[:].bitcast(I32), 0)

        nc.sync.dma_start(slots[:], offs)
        nc.sync.dma_start(picks[:], offs2)
        nc.sync.dma_start(out=w_raw[:], in_=w1.rearrange("(p t) r -> p t r", t=PACK))
        load_scales(tab_s, tab_scales, 0)
        tab_w = sb.tile([P, T], I32, name="tab_w", tag="first_words", align_bytes=64)
        load_words(tab_w, tab_words)

        ident = sb.tile([P, P], F32, name="ident")
        zeros = sb.tile([P, P], F32, name="zeros", tag="columns")
        nc.gpsimd.memset(zeros[:], 0.0)
        nc.gpsimd.affine_select(
            out=ident[:], in_=zeros[:], compare_op=ALU.not_equal, fill=1.0, base=0, pattern=[[-1, P]], channel_multiplier=1
        )

        warm_out = sb.tile([P, 1], F32, name="warm_out")
        nc.scalar.activation(out=warm_out[:], in_=eps[:], func=ACT.Abs_reciprocal_sqrt)

        columns = sb.tile([P, 2, 8], F32, name="columns", tag="columns")
        gain_col, pb_pairs = columns[:, 0, 0:1], columns[:, 1, 0:2]
        load_scales(dtab_s, dtab_scales, DTAB_FIRST)
        nc.sync.dma_start(out=gain_col, in_=gain)
        nc.sync.dma_start(out=pb_pairs, in_=pb[0].rearrange("(p c) -> p c", c=2))

        w_bf = sb.tile([P, R, PACK], BF16, name="w_bf", align_bytes=64)
        nc.vector.tensor_copy(out=w_bf[:], in_=w_raw[:].rearrange("p t r -> p r t"))
        dtab_w = sb.tile([P, T], I32, name="dtab_w", tag="late_words", align_bytes=64)
        load_words(dtab_w, dtab_words)
        w_codes = sb.tile([P, R], U32, name="w_codes", align_bytes=64)
        w_scales = sb.tile([P, R], U8, name="w_scales", align_bytes=64)

        tab_sg = sb.tile([P, J], U8, name="tab_sg", align_bytes=64)
        dtab_sg = sb.tile([P, J], U8, name="dtab_sg", align_bytes=64)
        tab_wg = sb.tile([P, J], U32, name="tab_wg", tag="first_picked", align_bytes=64)

        nc.vector.tensor_copy(tab_sg[:], tab_s[:].indirect(slots[:]))
        nc.vector.quantize_mx(
            out=w_codes[:].bitcast(FP8X4), scales=w_scales[:], in_=w_bf[:].rearrange("p r t -> p (r t)")
        )

        pb_ps = ps.tile([P, 2, P], F32, name="pb_ps")
        for c in range(2):
            nc.tensor.transpose(pb_ps[:, c, :], pb_pairs[:, c : c + 1].to_broadcast([P, P]), ident[:])
        nc.scalar.copy(out=pb_rows[:].rearrange("p (j c) -> p j c", c=2), in_=pb_ps[:].rearrange("p c j -> p j c"))

        h1 = sb.tile([P, J], F32, name="h1")
        xh1 = sb.tile([P, J], F32, name="xh1")

        def gather_words(dst, table, h):
            nc.vector.tensor_copy(dst[:, half(h, J)], table[:].bitcast(U32).indirect(slots[:, half(h, J // LIST_ROWS)]))

        def product(words, scales, h, name):
            acc = ps.tile([P, J // 2], F32, name=name)
            nc.tensor.matmul_mx(
                out=acc[:],
                lhsT=w_codes[:].bitcast(FP8X4),
                lhsT_scale=w_scales[:],
                rhs=words[:, half(h, J)].bitcast(FP8X4),
                rhs_scale=scales[:, half(h, J)],
                start=True,
                stop=True,
            )
            return acc

        for h in range(2):
            gather_words(tab_wg, tab_w, h)
            a_half = product(tab_wg, tab_sg[:], h, f"a_ps{h}")
            nc.scalar.activation(out=h1[:, half(h, J)], in_=a_half[:], func=ACT.Copy, scale=gain_col)

        og_col = sb.tile([P, 1], F32, name="og_col", tag="first_words", align_bytes=64)
        nc.sync.dma_start(out=og_col[:], in_=og)
        base_sb = sb.tile([P, M], F32, name="base_sb", tag="first_picked", align_bytes=64)
        nc.sync.dma_start(out=base_sb[:], in_=base)

        nc.vector.tensor_copy(dtab_sg[:], dtab_s[:].indirect(slots[:]))
        s = sb.tile([P, M], F32, name="s", tag="late_bytes", align_bytes=64)
        nc.vector.tensor_tensor(s[:], h1[:].indirect(picks[:]), pb_rows[:], ALU.add)
        sq = sb.tile([P, M], F32, name="sq")
        nc.scalar.activation(out=sq[:], in_=s[:], func=ACT.Square)
        dtab_wg = sb.tile([P, J], U32, name="dtab_wg", tag="bias_rows", align_bytes=64)
        gather_words(dtab_wg, dtab_w, 0)
        gather_words(dtab_wg, dtab_w, 1)
        ta_first = product(dtab_wg, dtab_sg[DTAB_FIRST:P, :], 0, "ta_ps0")
        nc.scalar.activation(out=xh1[:, half(0, J)], in_=ta_first[:], func=ACT.Copy, scale=gain_col)
        sq_sum = sb.tile([P, G], F32, name="sq_sum", tag="late_words", align_bytes=64)
        nc.vector.tensor_reduce(out=sq_sum[:], in_=grouped(sq), axis=AX.X, op=ALU.add)
        half_inv_q = sb.tile([P, M], F32, name="half_inv_q")
        nc.scalar.activation(
            out=grouped(half_inv_q), in_=spread(sq_sum), func=ACT.Abs_reciprocal_sqrt, scale=4.0 / GROUP, bias=eps[:]
        )
        ta_second = product(dtab_wg, dtab_sg[DTAB_FIRST:P, :], 1, "ta_ps1")
        nc.vector.tensor_scalar(out=xh1[:, half(1, J)], in0=ta_second[:], scalar1=gain_col, scalar2=None, op0=ALU.mult)

        u = sb.tile([P, M], F32, name="u")
        nc.vector.scalar_tensor_tensor(out=u[:], in0=s[:], scalar=2.0, in1=half_inv_q[:], op0=ALU.mult, op1=ALU.mult)
        silu_neg = sb.tile([P, M], F32, name="silu_neg")
        nc.scalar.activation(out=silu_neg[:], in_=u[:], func=ACT.Silu, scale=-1.0)
        tanh_half = sb.tile([P, M], F32, name="tanh_half")
        nc.scalar.activation(out=tanh_half[:], in_=u[:], func=ACT.Tanh, scale=0.5)

        xr = sb.tile([P, M], F32, name="xr")
        xr_u = sb.tile([P, M], F32, name="xr_u")
        xr_u_sum = sb.tile([P, G], F32, name="xr_u_sum")
        for h in range(2):
            nc.vector.tensor_tensor(
                xr[:, half(h, M)], xh1[:].indirect(picks[:, half(h, M // LIST_ROWS)]), half_inv_q[:, half(h, M)], ALU.mult
            )
        for h in range(2):
            nc.vector.tensor_tensor(xr_u[:, half(h, M)], xr[:, half(h, M)], u[:, half(h, M)], ALU.mult)
        for h in range(2):
            nc.vector.tensor_reduce(out=xr_u_sum[:, half(h, G)], in_=grouped(xr_u)[:, half(h, G), :], axis=AX.X, op=ALU.add)
        along_u = sb.tile([P, M], F32, name="along_u")
        neg_xu = sb.tile([P, M], F32, name="neg_xu")
        neg_slope = sb.tile([P, M], F32, name="neg_slope")
        xu1 = sb.tile([P, M], F32, name="xu1")
        res = sb.tile([P, M], F32, name="res")
        for h in range(2):
            nc.vector.scalar_tensor_tensor(
                out=grouped(along_u)[:, half(h, G), :],
                in0=grouped(u)[:, half(h, G), :],
                scalar=1.0 / GROUP,
                in1=spread(xr_u_sum)[:, half(h, G), :],
                op0=ALU.mult,
                op1=ALU.mult,
            )
        for h in range(2):
            nc.vector.tensor_tensor(neg_xu[:, half(h, M)], along_u[:, half(h, M)], xr[:, half(h, M)], ALU.subtract)
        tanh_plus_one = sb.tile([P, M], F32, name="tanh_plus_one")
        nc.scalar.activation(out=tanh_plus_one[:], in_=tanh_half[:], func=ACT.Identity, bias=1.0)
        nc.vector.scalar_tensor_tensor(
            out=neg_slope[:], in0=silu_neg[:], scalar=1.0, in1=tanh_plus_one[:], op0=ALU.subtract, op1=ALU.mult
        )
        for h in range(2):
            nc.vector.tensor_tensor(xu1[:, half(h, M)], neg_xu[:, half(h, M)], neg_slope[:, half(h, M)], ALU.mult)
        for h, queue in enumerate((nc.sync, nc.scalar)):
            cols = half(h, M)
            nc.vector.scalar_tensor_tensor(
                out=res[:, cols], in0=xu1[:, cols], scalar=og_col[:], in1=base_sb[:, cols], op0=ALU.mult, op1=ALU.add
            )
            queue.dma_start(out=out[:, cols], in_=res[:, cols])
